import numpy as np
import ml_dtypes

BF16 = ml_dtypes.bfloat16


def bf(x):
    return np.asarray(x, np.float32).astype(BF16)


def f32(x):
    return np.asarray(x, np.float32)


def f64(x):
    return np.asarray(x).astype(np.float64)


def striped(idx):
    return np.tile(idx.reshape(-1, 16).T, (8, 1))


S, K, M, N, B, Q = 256, 512, 128, 256, 4, 64


def setup_inputs():
    return {"base": bf(np.random.standard_normal((B, M, S))), "x": bf(np.random.standard_normal((K, N))), "w": bf(np.random.standard_normal((K, M)) / np.sqrt(K)), "b": f32(0.5 * np.random.standard_normal((M, 1))), "offs": striped(np.random.permutation(S))}


def reference(base, x, w, b, offs):
    idx = offs[:16].T.reshape(-1)
    z = f64(base).copy()
    for i in range(B):
        z[i][:, idx[i * Q : (i + 1) * Q]] += f64(w).T @ f64(x)[:, i * Q : (i + 1) * Q]
    return z + f64(b)

@@ -1,0 +1,60 @@
+import concourse.mybir as mybir
+from concourse.masks import make_identity
+
+BF16, F32, U16 = mybir.dt.bfloat16, mybir.dt.float32, mybir.dt.uint16
+
+P = 128
+SEQS = 4
+TOKENS = 256
+PIECE = 64
+KBLOCKS = 4
+OFFS_COLS = PIECE // 16
+
+FLOPS = 2 * (KBLOCKS * P) * P * (SEQS * PIECE)
+
+
+def tile_scatter_matmul_kernel(tc, base, x, w, b, offs, out):
+    nc = tc.nc
+    with (
+        tc.tile_pool(name="held", bufs=1) as held,
+        tc.psum_pool(name="banks", bufs=1) as banks,
+    ):
+        offsets = held.tile([P, SEQS * OFFS_COLS], U16, name="offsets")
+        nc.sync.dma_start(offsets[:], offs)
+
+        base_sb = held.tile([P, SEQS, TOKENS], BF16, name="base_sb")
+        nc.scalar.dma_start(base_sb[:], base.rearrange("i m t -> m i t"))
+
+        w_sb = held.tile([P, KBLOCKS, P], BF16, name="w_sb")
+        nc.sync.dma_start(w_sb[:], w.rearrange("(p kb) m -> p kb m", kb=KBLOCKS))
+        x_sb = held.tile([P, KBLOCKS, SEQS * PIECE], BF16, name="x_sb")
+        nc.sync.dma_start(x_sb[:], x.rearrange("(p kb) n -> p kb n", kb=KBLOCKS))
+
+        bias = held.tile([P, 1], F32, name="bias")
+        nc.scalar.dma_start(bias[:], b.rearrange("(a p) o -> p (a o)", p=P))
+
+        ident = held.tile([P, P], BF16, name="ident")
+        make_identity(nc, ident[:])
+
+        windows = [banks.tile([P, TOKENS], F32, name=f"window{i}") for i in range(SEQS)]
+        for i in range(SEQS):
+            nc.tensor.matmul(windows[i][:], ident[:], base_sb[:, i, :], start=True, stop=False)
+
+        for i in range(SEQS):
+            piece = offsets[:, i * OFFS_COLS : (i + 1) * OFFS_COLS]
+            for kb in range(KBLOCKS):
+                nc.tensor.matmul(
+                    windows[i][:].indirect(piece),
+                    w_sb[:, kb, :],
+                    x_sb[:, kb, i * PIECE : (i + 1) * PIECE],
+                    start=False,
+                    stop=(kb == KBLOCKS - 1),
+                )
+
+            z = held.tile([P, TOKENS], F32, name=f"z{i}")
+            if i % 2 == 0:
+                nc.vector.tensor_scalar_add(z[:], windows[i][:], bias[:, 0:1])
+                nc.sync.dma_start(out[i], z[:])
+            else:
+                nc.scalar.activation(z[:], windows[i][:], mybir.ActivationFunctionType.Identity, bias=bias[:, 0:1])
+                nc.scalar.dma_start(out[i], z[:])

@@ -22,13 +22,15 @@ def tile_scatter_matmul_kernel(tc, base, x, w, b, offs, out):
         offsets = held.tile([P, SEQS * OFFS_COLS], U16, name="offsets")
         nc.sync.dma_start(offsets[:], offs)
 
-        base_sb = held.tile([P, SEQS, TOKENS], BF16, name="base_sb")
-        nc.scalar.dma_start(base_sb[:], base.rearrange("i m t -> m i t"))
+        queues = [nc.sync, nc.scalar]
+        base_sb = [held.tile([P, TOKENS], BF16, name=f"base_sb{i}") for i in range(SEQS)]
+        for i in range(SEQS):
+            queues[i % 2].dma_start(base_sb[i][:], base[i])
 
         w_sb = held.tile([P, KBLOCKS, P], BF16, name="w_sb")
         nc.sync.dma_start(w_sb[:], w.rearrange("(p kb) m -> p kb m", kb=KBLOCKS))
         x_sb = held.tile([P, KBLOCKS, SEQS * PIECE], BF16, name="x_sb")
-        nc.sync.dma_start(x_sb[:], x.rearrange("(p kb) n -> p kb n", kb=KBLOCKS))
+        nc.scalar.dma_start(x_sb[:], x.rearrange("(p kb) n -> p kb n", kb=KBLOCKS))
 
         bias = held.tile([P, 1], F32, name="bias")
         nc.scalar.dma_start(bias[:], b.rearrange("(a p) o -> p (a o)", p=P))
@@ -38,7 +40,7 @@ def tile_scatter_matmul_kernel(tc, base, x, w, b, offs, out):
 
         windows = [banks.tile([P, TOKENS], F32, name=f"window{i}") for i in range(SEQS)]
         for i in range(SEQS):
-            nc.tensor.matmul(windows[i][:], ident[:], base_sb[:, i, :], start=True, stop=False)
+            nc.tensor.matmul(windows[i][:], ident[:], base_sb[i][:], start=True, stop=False)
 
         for i in range(SEQS):
             piece = offsets[:, i * OFFS_COLS : (i + 1) * OFFS_COLS]

@@ -9,6 +9,8 @@ TOKENS = 256
 PIECE = 64
 KBLOCKS = 4
 OFFS_COLS = PIECE // 16
+BANK = 512
+WARMUP = 4
 
 FLOPS = 2 * (KBLOCKS * P) * P * (SEQS * PIECE)
 
@@ -37,6 +39,12 @@ def tile_scatter_matmul_kernel(tc, base, x, w, b, offs, out):
 
         ident = held.tile([P, P], BF16, name="ident")
         make_identity(nc, ident[:])
+
+        zeros = held.tile([P, BANK], BF16, name="zeros")
+        nc.vector.memset(zeros[:], 0.0)
+        scratch = banks.tile([P, BANK], F32, name="scratch")
+        for _ in range(WARMUP):
+            nc.tensor.matmul(scratch[:], zeros[:, 0:P], zeros[:], start=True, stop=True)
 
         windows = [banks.tile([P, TOKENS], F32, name=f"window{i}") for i in range(SEQS)]
         for i in range(SEQS):

@@ -62,9 +62,5 @@ def tile_scatter_matmul_kernel(tc, base, x, w, b, offs, out):
                 )
 
             z = held.tile([P, TOKENS], F32, name=f"z{i}")
-            if i % 2 == 0:
-                nc.vector.tensor_scalar_add(z[:], windows[i][:], bias[:, 0:1])
-                nc.sync.dma_start(out[i], z[:])
-            else:
-                nc.scalar.activation(z[:], windows[i][:], mybir.ActivationFunctionType.Identity, bias=bias[:, 0:1])
-                nc.scalar.dma_start(out[i], z[:])
+            nc.vector.tensor_scalar_add(z[:], windows[i][:], bias[:, 0:1])
+            queues[i % 2].dma_start(out[i], z[:])

@@ -37,14 +37,16 @@ def tile_scatter_matmul_kernel(tc, base, x, w, b, offs, out):
         bias = held.tile([P, 1], F32, name="bias")
         nc.scalar.dma_start(bias[:], b.rearrange("(a p) o -> p (a o)", p=P))
 
+        zeros = held.tile([P, P], BF16, name="zeros")
+        nc.gpsimd.memset(zeros[:], 0.0)
+        scratch = banks.tile([P, BANK // P, P], F32, name="scratch")
+        for _ in range(WARMUP):
+            nc.tensor.matmul(
+                scratch[:], zeros[:], zeros[:].unsqueeze(1).to_broadcast([P, BANK // P, P]), start=True, stop=True
+            )
+
         ident = held.tile([P, P], BF16, name="ident")
         make_identity(nc, ident[:])
-
-        zeros = held.tile([P, BANK], BF16, name="zeros")
-        nc.vector.memset(zeros[:], 0.0)
-        scratch = banks.tile([P, BANK], F32, name="scratch")
-        for _ in range(WARMUP):
-            nc.tensor.matmul(scratch[:], zeros[:, 0:P], zeros[:], start=True, stop=True)
 
         windows = [banks.tile([P, TOKENS], F32, name=f"window{i}") for i in range(SEQS)]
         for i in range(SEQS):

import concourse.mybir as mybir
from concourse.masks import make_identity

BF16, F32, U16 = mybir.dt.bfloat16, mybir.dt.float32, mybir.dt.uint16

P = 128
SEQS = 4
TOKENS = 256
PIECE = 64
KBLOCKS = 4
OFFS_COLS = PIECE // 16
BANK = 512
WARMUP = 4

FLOPS = 2 * (KBLOCKS * P) * P * (SEQS * PIECE)


def tile_scatter_matmul_kernel(tc, base, x, w, b, offs, out):
    nc = tc.nc
    with (
        tc.tile_pool(name="held", bufs=1) as held,
        tc.psum_pool(name="banks", bufs=1) as banks,
    ):
        offsets = held.tile([P, SEQS * OFFS_COLS], U16, name="offsets")
        nc.sync.dma_start(offsets[:], offs)

        queues = [nc.sync, nc.scalar]
        base_sb = [held.tile([P, TOKENS], BF16, name=f"base_sb{i}") for i in range(SEQS)]
        for i in range(SEQS):
            queues[i % 2].dma_start(base_sb[i][:], base[i])

        w_sb = held.tile([P, KBLOCKS, P], BF16, name="w_sb")
        nc.sync.dma_start(w_sb[:], w.rearrange("(p kb) m -> p kb m", kb=KBLOCKS))
        x_sb = held.tile([P, KBLOCKS, SEQS * PIECE], BF16, name="x_sb")
        nc.scalar.dma_start(x_sb[:], x.rearrange("(p kb) n -> p kb n", kb=KBLOCKS))

        bias = held.tile([P, 1], F32, name="bias")
        nc.scalar.dma_start(bias[:], b.rearrange("(a p) o -> p (a o)", p=P))

        zeros = held.tile([P, P], BF16, name="zeros")
        nc.gpsimd.memset(zeros[:], 0.0)
        scratch = banks.tile([P, BANK // P, P], F32, name="scratch")
        for _ in range(WARMUP):
            nc.tensor.matmul(
                scratch[:], zeros[:], zeros[:].unsqueeze(1).to_broadcast([P, BANK // P, P]), start=True, stop=True
            )

        ident = held.tile([P, P], BF16, name="ident")
        make_identity(nc, ident[:])

        windows = [banks.tile([P, TOKENS], F32, name=f"window{i}") for i in range(SEQS)]
        for i in range(SEQS):
            nc.tensor.matmul(windows[i][:], ident[:], base_sb[i][:], start=True, stop=False)

        for i in range(SEQS):
            piece = offsets[:, i * OFFS_COLS : (i + 1) * OFFS_COLS]
            for kb in range(KBLOCKS):
                nc.tensor.matmul(
                    windows[i][:].indirect(piece),
                    w_sb[:, kb, :],
                    x_sb[:, kb, i * PIECE : (i + 1) * PIECE],
                    start=False,
                    stop=(kb == KBLOCKS - 1),
                )

            z = held.tile([P, TOKENS], F32, name=f"z{i}")
            nc.vector.tensor_scalar_add(z[:], windows[i][:], bias[:, 0:1])
            queues[i % 2].dma_start(out[i], z[:])
